import numpy as np
import ml_dtypes


def mxq(x, axis, fmt="e4m3"):
    dtype, down = {"e4m3": (ml_dtypes.float8_e4m3fn, 7), "e5m2": (ml_dtypes.float8_e5m2, 14)}[fmt]
    v = np.moveaxis(np.asarray(x, np.float32).astype(ml_dtypes.bfloat16).astype(np.float64), axis, -1)
    blocks = v.reshape(v.shape[:-1] + (-1, 32))
    amax = np.abs(blocks).max(-1, keepdims=True)
    byte = np.maximum(np.where(amax > 0, np.frexp(amax)[1] - 1 + 127, 0) - down, 1)
    scale = np.exp2(byte - 127.0)
    codes = (blocks / scale).astype(np.float32).astype(dtype).astype(np.float64)
    return np.moveaxis((codes * scale).reshape(v.shape), -1, axis)


WIDE = False


def mx_kscale(k):
    if not WIDE:
        return np.ones(k)
    levels = np.array([10, -10, 5, -5, 0])
    if k % 512:
        return np.exp2(np.random.permutation(np.resize(levels, k // 32))).repeat(32)
    a = np.empty((k // 512, 16))
    for p in range(k // 512):
        a[p, :8] = np.random.permutation(np.resize(levels, 8))
        for g in range(8):
            far = levels[np.abs(levels - a[p, g]) >= 10]
            a[p, g + 8] = far[np.random.randint(len(far))]
    return np.exp2(a.ravel()).repeat(32)


def f64(x):
    return np.asarray(x).astype(np.float64)


def striped8(idx):
    return np.asarray(idx).reshape(8, -1, 16).transpose(0, 2, 1).reshape(128, -1).astype(np.uint16)


def unstriped8(offs):
    return offs.reshape(8, 16, -1).transpose(0, 2, 1).reshape(8, -1).astype(np.int64)


def pick8(x, idx, run):
    r = np.arange(len(x))
    return x[r[:, None], idx[r % (8 * run) // run]]


E2M1 = np.array([0.0, 0.5, 1.0, 1.5, 2.0, 3.0, 4.0, 6.0, -0.0, -0.5, -1.0, -1.5, -2.0, -3.0, -4.0, -6.0])


def pack_weight(w, fmt):
    k, n = w.shape
    w = f64(np.asarray(w, np.float32).astype(ml_dtypes.bfloat16)).reshape(k // 32, 32, n)
    amax = np.abs(w).max(1)
    if fmt == "e4m3":
        byte = np.frexp(amax)[1] - 1 + 127 - 7
    else:
        mant, ex = np.frexp(amax / 6.0)
        byte = np.where(mant > 0.5, ex, ex - 1) + 127
    byte = np.clip(np.where(amax > 0, byte, 1), 1, 254)
    scaled = (w * np.exp2(127.0 - byte)[:, None, :]).reshape(k, n).astype(np.float32)
    by_word = np.ascontiguousarray(scaled.reshape(k // 512, 128, 4, n).transpose(0, 1, 3, 2))
    if fmt == "e4m3":
        words = by_word.astype(ml_dtypes.float8_e4m3fn).view(np.uint8)
    else:
        c = by_word.astype(ml_dtypes.float4_e2m1fn).view(np.uint8) & 0xF
        words = (c[..., 0::2] | (c[..., 1::2] << 4)).reshape(k // 512, 128, 2 * n)
    return np.ascontiguousarray(words), np.ascontiguousarray(byte.astype(np.uint8).reshape(k // 512, 16, n))


def unpack_weight(words, scales, fmt):
    g, _, n = scales.shape
    words = np.ascontiguousarray(words).reshape(g, 128, n, -1)
    if fmt == "e4m3":
        vals = words.view(ml_dtypes.float8_e4m3fn).astype(np.float64)
    else:
        nib = np.empty((g, 128, n, 4), np.uint8)
        nib[..., 0::2] = words & 0xF
        nib[..., 1::2] = words >> 4
        vals = E2M1[nib]
    vals = vals * np.repeat(np.exp2(scales.astype(np.float64) - 127.0), 8, axis=1)[..., None]
    return vals.transpose(0, 1, 3, 2).reshape(g * 512, n)


D, T, U, I, Q = 512, 1024, 1024, 512, 128


def setup_inputs():
    n = np.random.standard_normal
    idx = np.stack([np.random.permutation(T)[:I] for _ in range(8)])
    idx2 = np.stack([np.random.permutation(U)[:I] for _ in range(8)])
    idx3 = np.stack([np.random.permutation(U)[:I] for _ in range(8)])
    idx4 = np.stack([np.random.permutation(T)[:I] for _ in range(8)])
    idx5 = np.stack([np.random.permutation(T)[:I] for _ in range(8)])
    fd = mx_kscale(D)
    keysp = pack_weight(n((D, T)) / fd[:, None], "e2m1")
    notesp = pack_weight(n((D, U)) / fd[:, None], "e4m3")
    return {
        "query": (n((D, Q)) * 1.0 / np.sqrt(D) * fd[:, None]).astype(np.float32),
        "keys_words": keysp[0],
        "keys_scales": keysp[1],
        "notes_words": notesp[0],
        "notes_scales": notesp[1],
        "lam": (np.random.uniform(0.5, 1.5, (Q, 1))).astype(np.float32),
        "offs": striped8(idx),
        "offs2": striped8(idx2),
        "offs3": striped8(idx3),
        "offs4": striped8(idx4),
        "offs5": striped8(idx5),
    }


def reference(query, keys_words, keys_scales, notes_words, notes_scales, lam, offs, offs2, offs3, offs4, offs5):
    idx = unstriped8(offs)
    idx2 = unstriped8(offs2)
    idx3 = unstriped8(offs3)
    idx4 = unstriped8(offs4)
    idx5 = unstriped8(offs5)
    keysu = unpack_weight(keys_words, keys_scales, "e2m1")
    notesu = unpack_weight(notes_words, notes_scales, "e4m3")
    queryq = mxq(f64(query), 0, "e4m3")
    a = queryq.T @ keysu
    b = queryq.T @ notesu
    f1 = np.zeros((Q, U))
    f1[np.arange(Q)[:, None], idx2[np.arange(Q) % 128 // 16]] = pick8(a, idx, 16)
    cc = b + f1
    f2 = np.zeros((Q, T))
    f2[np.arange(Q)[:, None], idx4[np.arange(Q) % 128 // 16]] = pick8(cc, idx3, 16)
    dd = a + f2 * f64(lam)
    y = pick8(dd, idx5, 16)
    return y

@@ -1,0 +1,144 @@
+from contextlib import ExitStack
+
+import concourse.mybir as mybir
+
+D, T, U, I, Q = 512, 1024, 1024, 512, 128
+FLOPS = 2 * D * Q * (T + U)
+
+F32 = mybir.dt.float32
+BF16 = mybir.dt.bfloat16
+I32 = mybir.dt.int32
+U32 = mybir.dt.uint32
+U16 = mybir.dt.uint16
+U8 = mybir.dt.uint8
+FP8X4 = mybir.dt.float8_e4m3fn_x4
+FP4X4 = mybir.dt.float4_e2m1fn_x4
+MULT = mybir.AluOpType.mult
+ADD = mybir.AluOpType.add
+COPY = mybir.ActivationFunctionType.Copy
+
+P = 128
+PACK = 4
+BANK = 512
+A_WIDTHS = (512, 256, 128, 128)
+HALF = I // 2
+
+
+def load_scale_rows(queue, plane, rows):
+    for quadrant in range(4):
+        queue.dma_start(
+            out=plane[32 * quadrant : 32 * quadrant + 4, :].bitcast(I32),
+            in_=rows[0, 4 * quadrant : 4 * quadrant + 4, :].bitcast(I32),
+        )
+
+
+def gather_halves(nc, picked, window, offsets):
+    cols = HALF // 16
+    nc.vector.tensor_copy(picked[0][:], window[:].indirect(offsets[:, 0:cols]))
+    nc.scalar.activation(picked[1][:], window[:].indirect(offsets[:, cols : 2 * cols]), COPY)
+
+
+def scatter_halves(nc, window, offsets, picked):
+    cols = HALF // 16
+    for h in range(2):
+        nc.vector.tensor_copy(window[:].indirect(offsets[:, h * cols : (h + 1) * cols]), picked[h][:])
+
+
+def tile_attend_thereandback_two_kernel(
+    tc, query, keys_words, keys_scales, notes_words, notes_scales, lam, offs, offs2, offs3, offs4, offs5, out
+):
+    nc = tc.nc
+    with ExitStack() as ctx:
+        sb = ctx.enter_context(tc.tile_pool(name="sb", bufs=1))
+        psum = ctx.enter_context(tc.psum_pool(name="psum", bufs=1))
+
+        lists = [sb.tile([P, I // 16], U16, name=f"list{n}") for n in range(5)]
+        q_raw = sb.tile([P, PACK, Q], F32)
+        q_bf = sb.tile([P, Q, PACK], BF16, align_bytes=64)
+        q_codes = sb.tile([P, Q], U32, align_bytes=64)
+        q_plane = sb.tile([P, Q], U8, align_bytes=64)
+        k_words = sb.tile([P, 2 * T], U8, align_bytes=64)
+        k_plane = sb.tile([P, T], U8, align_bytes=64)
+        n_words = sb.tile([P, U], U32, align_bytes=64)
+        n_plane = sb.tile([P, U], U8, align_bytes=64)
+        lam_sb = sb.tile([P, 1], F32)
+        a_sb = sb.tile([P, T], F32)
+        f1 = sb.tile([P, U], F32)
+        cc = sb.tile([P, U], F32)
+        f2 = sb.tile([P, T], F32)
+        dd = sb.tile([P, T], F32)
+        g1 = [sb.tile([P, HALF], F32, name=f"g1_{h}") for h in range(2)]
+        g2 = [sb.tile([P, HALF], F32, name=f"g2_{h}") for h in range(2)]
+        y = [sb.tile([P, HALF], F32, name=f"y_{h}") for h in range(2)]
+
+        nc.vector.memset(k_plane[:].bitcast(I32), 0)
+        nc.sync.dma_start(out=q_raw[:], in_=query.rearrange("(p j) q -> p j q", j=PACK))
+        load_scale_rows(nc.scalar, k_plane, keys_scales)
+        nc.sync.dma_start(out=k_words[:].bitcast(I32), in_=keys_words[0].bitcast(I32))
+        nc.sync.dma_start(lists[0][:], offs)
+        nc.sync.dma_start(lists[1][:], offs2)
+        nc.vector.memset(n_plane[:].bitcast(I32), 0)
+        nc.vector.memset(f1[:], 0.0)
+        nc.vector.memset(f2[:], 0.0)
+        nc.sync.dma_start(
+            out=n_words[:].bitcast(I32), in_=notes_words[0].rearrange("p n t -> p (n t)").bitcast(I32)
+        )
+        load_scale_rows(nc.sync, n_plane, notes_scales)
+        nc.sync.dma_start(lists[2][:], offs3)
+        nc.sync.dma_start(lists[3][:], offs4)
+        nc.sync.dma_start(lists[4][:], offs5)
+        nc.sync.dma_start(out=lam_sb[:], in_=lam)
+
+        nc.vector.tensor_copy(out=q_bf[:], in_=q_raw[:].rearrange("p j q -> p q j"))
+        nc.vector.quantize_mx(
+            out=q_codes[:].bitcast(FP8X4), scales=q_plane[:], in_=q_bf[:].rearrange("p q j -> p (q j)")
+        )
+
+        a_banks = []
+        start = 0
+        for n, width in enumerate(A_WIDTHS):
+            bank = psum.tile([P, width], F32, name=f"a_bank{n}")
+            nc.tensor.matmul_mx(
+                out=bank[:],
+                lhsT=q_codes[:].bitcast(FP8X4),
+                lhsT_scale=q_plane[:],
+                rhs=k_words[:, 2 * start : 2 * (start + width)].bitcast(FP4X4),
+                rhs_scale=k_plane[:, start : start + width],
+                start=True,
+                stop=True,
+            )
+            if n in (0, 3):
+                nc.scalar.copy(a_sb[:, start : start + width], bank[:])
+            else:
+                nc.vector.tensor_copy(a_sb[:, start : start + width], bank[:])
+            a_banks.append(bank)
+            start += width
+
+        b_banks = []
+        for n in range(U // BANK):
+            bank = psum.tile([P, BANK], F32, name=f"b_bank{n}")
+            cols = slice(n * BANK, (n + 1) * BANK)
+            nc.tensor.matmul_mx(
+                out=bank[:],
+                lhsT=q_codes[:].bitcast(FP8X4),
+                lhsT_scale=q_plane[:],
+                rhs=n_words[:, cols].bitcast(FP8X4),
+                rhs_scale=n_plane[:, cols],
+                start=True,
+                stop=True,
+            )
+            b_banks.append(bank)
+
+        gather_halves(nc, g1, a_sb, lists[0])
+        scatter_halves(nc, f1, lists[1], g1)
+        for n in range(U // BANK):
+            cols = slice(n * BANK, (n + 1) * BANK)
+            nc.vector.tensor_tensor(cc[:, cols], b_banks[n][:], f1[:, cols], ADD)
+
+        gather_halves(nc, g2, cc, lists[2])
+        scatter_halves(nc, f2, lists[3], g2)
+        nc.vector.scalar_tensor_tensor(dd[:], f2[:], lam_sb[:], a_sb[:], MULT, ADD)
+
+        gather_halves(nc, y, dd, lists[4])
+        nc.sync.dma_start(out=out[:, 0:HALF], in_=y[0][:])
+        nc.scalar.dma_start(out=out[:, HALF:I], in_=y[1][:])

@@ -21,6 +21,7 @@ P = 128
 PACK = 4
 BANK = 512
 A_WIDTHS = (512, 256, 128, 128)
+SPLIT = 704
 HALF = I // 2
 
 
@@ -32,16 +33,10 @@ def load_scale_rows(queue, plane, rows):
         )
 
 
-def gather_halves(nc, picked, window, offsets):
+def gather_halves(nc, low, high, window, offsets):
     cols = HALF // 16
-    nc.vector.tensor_copy(picked[0][:], window[:].indirect(offsets[:, 0:cols]))
-    nc.scalar.activation(picked[1][:], window[:].indirect(offsets[:, cols : 2 * cols]), COPY)
-
-
-def scatter_halves(nc, window, offsets, picked):
-    cols = HALF // 16
-    for h in range(2):
-        nc.vector.tensor_copy(window[:].indirect(offsets[:, h * cols : (h + 1) * cols]), picked[h][:])
+    nc.vector.tensor_copy(low, window[:].indirect(offsets[:, 0:cols]))
+    nc.scalar.activation(high, window[:].indirect(offsets[:, cols : 2 * cols]), COPY)
 
 
 def tile_attend_thereandback_two_kernel(
@@ -67,8 +62,8 @@ def tile_attend_thereandback_two_kernel(
         cc = sb.tile([P, U], F32)
         f2 = sb.tile([P, T], F32)
         dd = sb.tile([P, T], F32)
-        g1 = [sb.tile([P, HALF], F32, name=f"g1_{h}") for h in range(2)]
-        g2 = [sb.tile([P, HALF], F32, name=f"g2_{h}") for h in range(2)]
+        g1 = sb.tile([P, I], F32)
+        g2 = sb.tile([P, I], F32)
         y = [sb.tile([P, HALF], F32, name=f"y_{h}") for h in range(2)]
 
         nc.vector.memset(k_plane[:].bitcast(I32), 0)
@@ -89,10 +84,16 @@ def tile_attend_thereandback_two_kernel(
         nc.sync.dma_start(lists[4][:], offs5)
         nc.sync.dma_start(out=lam_sb[:], in_=lam)
 
-        nc.vector.tensor_copy(out=q_bf[:], in_=q_raw[:].rearrange("p j q -> p q j"))
-        nc.vector.quantize_mx(
-            out=q_codes[:].bitcast(FP8X4), scales=q_plane[:], in_=q_bf[:].rearrange("p q j -> p (q j)")
-        )
+        for h in range(2):
+            cols = slice(h * Q // 2, (h + 1) * Q // 2)
+            nc.vector.tensor_copy(out=q_bf[:, cols, :], in_=q_raw[:, :, cols].rearrange("p j q -> p q j"))
+        for h in range(2):
+            cols = slice(h * Q // 2, (h + 1) * Q // 2)
+            nc.vector.quantize_mx(
+                out=q_codes[:, cols].bitcast(FP8X4),
+                scales=q_plane[:, cols],
+                in_=q_bf[:, cols, :].rearrange("p q j -> p (q j)"),
+            )
 
         a_banks = []
         start = 0
@@ -129,16 +130,23 @@ def tile_attend_thereandback_two_kernel(
             )
             b_banks.append(bank)
 
-        gather_halves(nc, g1, a_sb, lists[0])
-        scatter_halves(nc, f1, lists[1], g1)
-        for n in range(U // BANK):
-            cols = slice(n * BANK, (n + 1) * BANK)
-            nc.vector.tensor_tensor(cc[:, cols], b_banks[n][:], f1[:, cols], ADD)
+        b_tail = sb.tile([P, U - SPLIT], F32)
+        nc.scalar.copy(b_tail[:], b_banks[1][:, SPLIT - BANK : BANK])
+        lam_wide = sb.tile([P, I], F32)
+        nc.scalar.copy(lam_wide[:], lam_sb[:].to_broadcast([P, I]))
 
-        gather_halves(nc, g2, cc, lists[2])
-        scatter_halves(nc, f2, lists[3], g2)
-        nc.vector.scalar_tensor_tensor(dd[:], f2[:], lam_sb[:], a_sb[:], MULT, ADD)
+        gather_halves(nc, g1[:, 0:HALF], g1[:, HALF:I], a_sb, lists[0])
+        nc.vector.tensor_copy(f1[:].indirect(lists[1][:]), g1[:])
+        nc.gpsimd.tensor_tensor(cc[:, SPLIT:U], b_tail[:], f1[:, SPLIT:U], ADD)
+        nc.vector.tensor_tensor(cc[:, 0:BANK], b_banks[0][:], f1[:, 0:BANK], ADD)
+        nc.vector.tensor_tensor(cc[:, BANK:SPLIT], b_banks[1][:, 0 : SPLIT - BANK], f1[:, BANK:SPLIT], ADD)
 
-        gather_halves(nc, y, dd, lists[4])
+        gather_halves(nc, g2[:, 0:HALF], g2[:, HALF:I], cc, lists[2])
+        nc.vector.tensor_tensor(f2[:].indirect(lists[3][:]), g2[:], lam_wide[:], MULT)
+        nc.gpsimd.tensor_tensor(dd[:, SPLIT:T], a_sb[:, SPLIT:T], f2[:, SPLIT:T], ADD)
+        nc.vector.tensor_tensor(dd[:, 0:BANK], a_banks[0][:], f2[:, 0:BANK], ADD)
+        nc.vector.tensor_tensor(dd[:, BANK:SPLIT], a_banks[1][:, 0 : SPLIT - BANK], f2[:, BANK:SPLIT], ADD)
+
+        gather_halves(nc, y[0][:], y[1][:], dd, lists[4])
         nc.sync.dma_start(out=out[:, 0:HALF], in_=y[0][:])
         nc.scalar.dma_start(out=out[:, HALF:I], in_=y[1][:])

@@ -79,10 +79,10 @@ def tile_attend_thereandback_two_kernel(
             out=n_words[:].bitcast(I32), in_=notes_words[0].rearrange("p n t -> p (n t)").bitcast(I32)
         )
         load_scale_rows(nc.sync, n_plane, notes_scales)
+        nc.sync.dma_start(out=lam_sb[:], in_=lam)
         nc.sync.dma_start(lists[2][:], offs3)
         nc.sync.dma_start(lists[3][:], offs4)
         nc.sync.dma_start(lists[4][:], offs5)
-        nc.sync.dma_start(out=lam_sb[:], in_=lam)
 
         for h in range(2):
             cols = slice(h * Q // 2, (h + 1) * Q // 2)

@@ -20,13 +20,13 @@ COPY = mybir.ActivationFunctionType.Copy
 P = 128
 PACK = 4
 BANK = 512
-A_WIDTHS = (512, 256, 128, 128)
+A_WIDTHS = (256, 256, 256, 128, 128)
 SPLIT = 704
 HALF = I // 2
 
 
-def load_scale_rows(queue, plane, rows):
-    for quadrant in range(4):
+def load_scale_rows(queues, plane, rows):
+    for quadrant, queue in enumerate(queues):
         queue.dma_start(
             out=plane[32 * quadrant : 32 * quadrant + 4, :].bitcast(I32),
             in_=rows[0, 4 * quadrant : 4 * quadrant + 4, :].bitcast(I32),
@@ -68,7 +68,7 @@ def tile_attend_thereandback_two_kernel(
 
         nc.vector.memset(k_plane[:].bitcast(I32), 0)
         nc.sync.dma_start(out=q_raw[:], in_=query.rearrange("(p j) q -> p j q", j=PACK))
-        load_scale_rows(nc.scalar, k_plane, keys_scales)
+        load_scale_rows((nc.sync, nc.scalar, nc.sync, nc.scalar), k_plane, keys_scales)
         nc.sync.dma_start(out=k_words[:].bitcast(I32), in_=keys_words[0].bitcast(I32))
         nc.sync.dma_start(lists[0][:], offs)
         nc.sync.dma_start(lists[1][:], offs2)
@@ -78,7 +78,7 @@ def tile_attend_thereandback_two_kernel(
         nc.sync.dma_start(
             out=n_words[:].bitcast(I32), in_=notes_words[0].rearrange("p n t -> p (n t)").bitcast(I32)
         )
-        load_scale_rows(nc.sync, n_plane, notes_scales)
+        load_scale_rows((nc.sync,) * 4, n_plane, notes_scales)
         nc.sync.dma_start(out=lam_sb[:], in_=lam)
         nc.sync.dma_start(lists[2][:], offs3)
         nc.sync.dma_start(lists[3][:], offs4)
@@ -108,15 +108,15 @@ def tile_attend_thereandback_two_kernel(
                 start=True,
                 stop=True,
             )
-            if n in (0, 3):
+            if n % 2 == 0:
                 nc.scalar.copy(a_sb[:, start : start + width], bank[:])
             else:
                 nc.vector.tensor_copy(a_sb[:, start : start + width], bank[:])
             a_banks.append(bank)
             start += width
 
-        b_banks = []
-        for n in range(U // BANK):
+        b_banks = {}
+        for n in reversed(range(U // BANK)):
             bank = psum.tile([P, BANK], F32, name=f"b_bank{n}")
             cols = slice(n * BANK, (n + 1) * BANK)
             nc.tensor.matmul_mx(
@@ -128,7 +128,7 @@ def tile_attend_thereandback_two_kernel(
                 start=True,
                 stop=True,
             )
-            b_banks.append(bank)
+            b_banks[n] = bank
 
         b_tail = sb.tile([P, U - SPLIT], F32)
         nc.scalar.copy(b_tail[:], b_banks[1][:, SPLIT - BANK : BANK])
@@ -144,8 +144,9 @@ def tile_attend_thereandback_two_kernel(
         gather_halves(nc, g2[:, 0:HALF], g2[:, HALF:I], cc, lists[2])
         nc.vector.tensor_tensor(f2[:].indirect(lists[3][:]), g2[:], lam_wide[:], MULT)
         nc.gpsimd.tensor_tensor(dd[:, SPLIT:T], a_sb[:, SPLIT:T], f2[:, SPLIT:T], ADD)
-        nc.vector.tensor_tensor(dd[:, 0:BANK], a_banks[0][:], f2[:, 0:BANK], ADD)
-        nc.vector.tensor_tensor(dd[:, BANK:SPLIT], a_banks[1][:, 0 : SPLIT - BANK], f2[:, BANK:SPLIT], ADD)
+        for n in range(3):
+            lo, hi = 256 * n, min(256 * (n + 1), SPLIT)
+            nc.vector.tensor_tensor(dd[:, lo:hi], a_banks[n][:, 0 : hi - lo], f2[:, lo:hi], ADD)
 
         gather_halves(nc, y[0][:], y[1][:], dd, lists[4])
         nc.sync.dma_start(out=out[:, 0:HALF], in_=y[0][:])

from contextlib import ExitStack

import concourse.mybir as mybir

D, T, U, I, Q = 512, 1024, 1024, 512, 128
FLOPS = 2 * D * Q * (T + U)

F32 = mybir.dt.float32
BF16 = mybir.dt.bfloat16
I32 = mybir.dt.int32
U32 = mybir.dt.uint32
U16 = mybir.dt.uint16
U8 = mybir.dt.uint8
FP8X4 = mybir.dt.float8_e4m3fn_x4
FP4X4 = mybir.dt.float4_e2m1fn_x4
MULT = mybir.AluOpType.mult
ADD = mybir.AluOpType.add
COPY = mybir.ActivationFunctionType.Copy

P = 128
PACK = 4
BANK = 512
A_WIDTHS = (256, 256, 256, 128, 128)
SPLIT = 704
HALF = I // 2


def load_scale_rows(queues, plane, rows):
    for quadrant, queue in enumerate(queues):
        queue.dma_start(
            out=plane[32 * quadrant : 32 * quadrant + 4, :].bitcast(I32),
            in_=rows[0, 4 * quadrant : 4 * quadrant + 4, :].bitcast(I32),
        )


def gather_halves(nc, low, high, window, offsets):
    cols = HALF // 16
    nc.vector.tensor_copy(low, window[:].indirect(offsets[:, 0:cols]))
    nc.scalar.activation(high, window[:].indirect(offsets[:, cols : 2 * cols]), COPY)


def tile_attend_thereandback_two_kernel(
    tc, query, keys_words, keys_scales, notes_words, notes_scales, lam, offs, offs2, offs3, offs4, offs5, out
):
    nc = tc.nc
    with ExitStack() as ctx:
        sb = ctx.enter_context(tc.tile_pool(name="sb", bufs=1))
        psum = ctx.enter_context(tc.psum_pool(name="psum", bufs=1))

        lists = [sb.tile([P, I // 16], U16, name=f"list{n}") for n in range(5)]
        q_raw = sb.tile([P, PACK, Q], F32)
        q_bf = sb.tile([P, Q, PACK], BF16, align_bytes=64)
        q_codes = sb.tile([P, Q], U32, align_bytes=64)
        q_plane = sb.tile([P, Q], U8, align_bytes=64)
        k_words = sb.tile([P, 2 * T], U8, align_bytes=64)
        k_plane = sb.tile([P, T], U8, align_bytes=64)
        n_words = sb.tile([P, U], U32, align_bytes=64)
        n_plane = sb.tile([P, U], U8, align_bytes=64)
        lam_sb = sb.tile([P, 1], F32)
        a_sb = sb.tile([P, T], F32)
        f1 = sb.tile([P, U], F32)
        cc = sb.tile([P, U], F32)
        f2 = sb.tile([P, T], F32)
        dd = sb.tile([P, T], F32)
        g1 = sb.tile([P, I], F32)
        g2 = sb.tile([P, I], F32)
        y = [sb.tile([P, HALF], F32, name=f"y_{h}") for h in range(2)]

        nc.vector.memset(k_plane[:].bitcast(I32), 0)
        nc.sync.dma_start(out=q_raw[:], in_=query.rearrange("(p j) q -> p j q", j=PACK))
        load_scale_rows((nc.sync, nc.scalar, nc.sync, nc.scalar), k_plane, keys_scales)
        nc.sync.dma_start(out=k_words[:].bitcast(I32), in_=keys_words[0].bitcast(I32))
        nc.sync.dma_start(lists[0][:], offs)
        nc.sync.dma_start(lists[1][:], offs2)
        nc.vector.memset(n_plane[:].bitcast(I32), 0)
        nc.vector.memset(f1[:], 0.0)
        nc.vector.memset(f2[:], 0.0)
        nc.sync.dma_start(
            out=n_words[:].bitcast(I32), in_=notes_words[0].rearrange("p n t -> p (n t)").bitcast(I32)
        )
        load_scale_rows((nc.sync,) * 4, n_plane, notes_scales)
        nc.sync.dma_start(out=lam_sb[:], in_=lam)
        nc.sync.dma_start(lists[2][:], offs3)
        nc.sync.dma_start(lists[3][:], offs4)
        nc.sync.dma_start(lists[4][:], offs5)

        for h in range(2):
            cols = slice(h * Q // 2, (h + 1) * Q // 2)
            nc.vector.tensor_copy(out=q_bf[:, cols, :], in_=q_raw[:, :, cols].rearrange("p j q -> p q j"))
        for h in range(2):
            cols = slice(h * Q // 2, (h + 1) * Q // 2)
            nc.vector.quantize_mx(
                out=q_codes[:, cols].bitcast(FP8X4),
                scales=q_plane[:, cols],
                in_=q_bf[:, cols, :].rearrange("p q j -> p (q j)"),
            )

        a_banks = []
        start = 0
        for n, width in enumerate(A_WIDTHS):
            bank = psum.tile([P, width], F32, name=f"a_bank{n}")
            nc.tensor.matmul_mx(
                out=bank[:],
                lhsT=q_codes[:].bitcast(FP8X4),
                lhsT_scale=q_plane[:],
                rhs=k_words[:, 2 * start : 2 * (start + width)].bitcast(FP4X4),
                rhs_scale=k_plane[:, start : start + width],
                start=True,
                stop=True,
            )
            if n % 2 == 0:
                nc.scalar.copy(a_sb[:, start : start + width], bank[:])
            else:
                nc.vector.tensor_copy(a_sb[:, start : start + width], bank[:])
            a_banks.append(bank)
            start += width

        b_banks = {}
        for n in reversed(range(U // BANK)):
            bank = psum.tile([P, BANK], F32, name=f"b_bank{n}")
            cols = slice(n * BANK, (n + 1) * BANK)
            nc.tensor.matmul_mx(
                out=bank[:],
                lhsT=q_codes[:].bitcast(FP8X4),
                lhsT_scale=q_plane[:],
                rhs=n_words[:, cols].bitcast(FP8X4),
                rhs_scale=n_plane[:, cols],
                start=True,
                stop=True,
            )
            b_banks[n] = bank

        b_tail = sb.tile([P, U - SPLIT], F32)
        nc.scalar.copy(b_tail[:], b_banks[1][:, SPLIT - BANK : BANK])
        lam_wide = sb.tile([P, I], F32)
        nc.scalar.copy(lam_wide[:], lam_sb[:].to_broadcast([P, I]))

        gather_halves(nc, g1[:, 0:HALF], g1[:, HALF:I], a_sb, lists[0])
        nc.vector.tensor_copy(f1[:].indirect(lists[1][:]), g1[:])
        nc.gpsimd.tensor_tensor(cc[:, SPLIT:U], b_tail[:], f1[:, SPLIT:U], ADD)
        nc.vector.tensor_tensor(cc[:, 0:BANK], b_banks[0][:], f1[:, 0:BANK], ADD)
        nc.vector.tensor_tensor(cc[:, BANK:SPLIT], b_banks[1][:, 0 : SPLIT - BANK], f1[:, BANK:SPLIT], ADD)

        gather_halves(nc, g2[:, 0:HALF], g2[:, HALF:I], cc, lists[2])
        nc.vector.tensor_tensor(f2[:].indirect(lists[3][:]), g2[:], lam_wide[:], MULT)
        nc.gpsimd.tensor_tensor(dd[:, SPLIT:T], a_sb[:, SPLIT:T], f2[:, SPLIT:T], ADD)
        for n in range(3):
            lo, hi = 256 * n, min(256 * (n + 1), SPLIT)
            nc.vector.tensor_tensor(dd[:, lo:hi], a_banks[n][:, 0 : hi - lo], f2[:, lo:hi], ADD)

        gather_halves(nc, y[0][:], y[1][:], dd, lists[4])
        nc.sync.dma_start(out=out[:, 0:HALF], in_=y[0][:])
        nc.scalar.dma_start(out=out[:, HALF:I], in_=y[1][:])
